import numpy as np
import ml_dtypes


def mxq(x, axis, fmt="e4m3"):
    dtype, down = {"e4m3": (ml_dtypes.float8_e4m3fn, 7), "e5m2": (ml_dtypes.float8_e5m2, 14)}[fmt]
    v = np.moveaxis(np.asarray(x, np.float32).astype(ml_dtypes.bfloat16).astype(np.float64), axis, -1)
    blocks = v.reshape(v.shape[:-1] + (-1, 32))
    amax = np.abs(blocks).max(-1, keepdims=True)
    byte = np.maximum(np.where(amax > 0, np.frexp(amax)[1] - 1 + 127, 0) - down, 1)
    scale = np.exp2(byte - 127.0)
    codes = (blocks / scale).astype(np.float32).astype(dtype).astype(np.float64)
    return np.moveaxis((codes * scale).reshape(v.shape), -1, axis)


WIDE = False


def mx_kscale(k):
    if not WIDE:
        return np.ones(k)
    levels = np.array([10, -10, 5, -5, 0])
    if k % 512:
        return np.exp2(np.random.permutation(np.resize(levels, k // 32))).repeat(32)
    a = np.empty((k // 512, 16))
    for p in range(k // 512):
        a[p, :8] = np.random.permutation(np.resize(levels, 8))
        for g in range(8):
            far = levels[np.abs(levels - a[p, g]) >= 10]
            a[p, g + 8] = far[np.random.randint(len(far))]
    return np.exp2(a.ravel()).repeat(32)


def f64(x):
    return np.asarray(x).astype(np.float64)


def striped(idx):
    return np.tile(np.asarray(idx).reshape(-1, 16).T, (8, 1)).astype(np.uint16)


def unstriped(offs):
    return offs[:16].T.reshape(-1).astype(np.int64)


E2M1 = np.array([0.0, 0.5, 1.0, 1.5, 2.0, 3.0, 4.0, 6.0, -0.0, -0.5, -1.0, -1.5, -2.0, -3.0, -4.0, -6.0])


def pack_weight(w, fmt):
    k, n = w.shape
    w = f64(np.asarray(w, np.float32).astype(ml_dtypes.bfloat16)).reshape(k // 32, 32, n)
    amax = np.abs(w).max(1)
    if fmt == "e4m3":
        byte = np.frexp(amax)[1] - 1 + 127 - 7
    else:
        mant, ex = np.frexp(amax / 6.0)
        byte = np.where(mant > 0.5, ex, ex - 1) + 127
    byte = np.clip(np.where(amax > 0, byte, 1), 1, 254)
    scaled = (w * np.exp2(127.0 - byte)[:, None, :]).reshape(k, n).astype(np.float32)
    by_word = np.ascontiguousarray(scaled.reshape(k // 512, 128, 4, n).transpose(0, 1, 3, 2))
    if fmt == "e4m3":
        words = by_word.astype(ml_dtypes.float8_e4m3fn).view(np.uint8)
    else:
        c = by_word.astype(ml_dtypes.float4_e2m1fn).view(np.uint8) & 0xF
        words = (c[..., 0::2] | (c[..., 1::2] << 4)).reshape(k // 512, 128, 2 * n)
    return np.ascontiguousarray(words), np.ascontiguousarray(byte.astype(np.uint8).reshape(k // 512, 16, n))


def unpack_weight(words, scales, fmt):
    g, _, n = scales.shape
    words = np.ascontiguousarray(words).reshape(g, 128, n, -1)
    if fmt == "e4m3":
        vals = words.view(ml_dtypes.float8_e4m3fn).astype(np.float64)
    else:
        nib = np.empty((g, 128, n, 4), np.uint8)
        nib[..., 0::2] = words & 0xF
        nib[..., 1::2] = words >> 4
        vals = E2M1[nib]
    vals = vals * np.repeat(np.exp2(scales.astype(np.float64) - 127.0), 8, axis=1)[..., None]
    return vals.transpose(0, 1, 3, 2).reshape(g * 512, n)


D, T, I, Q, E, G = 512, 2048, 512, 256, 512, 64


def setup_inputs():
    n = np.random.standard_normal
    idx = np.random.permutation(T)[:I]
    fd = mx_kscale(D)
    fi = mx_kscale(I)
    ti = np.ones(T)
    ti[idx] = fi
    keysp = pack_weight(n((D, T)) / fd[:, None], "e4m3")
    return {
        "query": (n((D, Q)) * 0.7 / np.sqrt(D) * fd[:, None]).astype(np.float32),
        "query2": (n((D, Q)) * 0.7 / np.sqrt(D) * fd[:, None]).astype(np.float32),
        "keys_words": keysp[0],
        "keys_scales": keysp[1],
        "xmark": np.tile(np.random.uniform(-1.0, 1.0, T), (128, 1)).astype(np.float32),
        "ymark": np.tile(np.random.uniform(-1.0, 1.0, T), (128, 1)).astype(np.float32),
        "lam": (np.random.uniform(0.5, 1.2, (Q, 1))).astype(np.float32),
        "os": (np.random.uniform(4.0, 16.0, (1, I)) * fi).astype(np.float32),
        "vals": (n((E, T)) / ti).astype(np.float32),
        "memq": (np.random.uniform(0.3, 1.0, (1, Q))).astype(np.float32),
        "offs": striped(idx),
    }


def reference(query, query2, keys_words, keys_scales, xmark, ymark, lam, os, vals, memq, offs):
    idx = unstriped(offs)
    keysu = unpack_weight(keys_words, keys_scales, "e4m3")
    queryq = mxq(f64(query), 0, "e4m3")
    keysidxg = keysu[:, idx]
    a = queryq.T @ keysidxg
    query2q = mxq(f64(query2), 0, "e4m3")
    b = query2q.T @ keysidxg
    dx = a - f64(xmark)[:1][:, idx]
    dy = b - f64(ymark)[:1][:, idx]
    s = (np.square(dx) + np.square(dy)) * f64(lam) * (-1.0)
    p = np.exp(s)
    pg = p.reshape(Q, G, I // G).sum(axis=2)
    rt0 = np.sqrt(pg)
    k0 = rt0 / np.sum(rt0, axis=1, keepdims=True) / np.square(pg)
    kr = np.repeat(k0, I // G, axis=1)
    w = np.square(p) * kr
    wo1 = w * f64(os)
    wt1 = wo1.T
    vt1 = f64(vals)[:, idx].T
    vt1q = mxq(vt1, 0, "e4m3")
    wt1q = mxq(wt1, 0, "e4m3")
    o = vt1q.T @ wt1q
    o1 = np.pad(o, ((0, 0), (1, 0)))[:, :Q]
    y = o - o1 * f64(memq)
    return y

@@ -1,0 +1,276 @@
+from contextlib import ExitStack
+
+import concourse.mybir as mybir
+from concourse.masks import make_identity
+
+F32 = mybir.dt.float32
+BF16 = mybir.dt.bfloat16
+I32 = mybir.dt.int32
+U32 = mybir.dt.uint32
+U16 = mybir.dt.uint16
+U8 = mybir.dt.uint8
+FP8X4 = mybir.dt.float8_e4m3fn_x4
+ACT = mybir.ActivationFunctionType
+ALU = mybir.AluOpType
+AXIS = mybir.AxisListType
+
+D, T, I, Q, E, G = 512, 2048, 512, 256, 512, 64
+P = 128
+PACK = 4
+RUN = I // G
+BANK = 512
+QT = Q // P
+IT = I // P
+ET = E // P
+
+FLOPS = 2 * 2 * D * Q * I + 2 * I * E * Q
+BYTES = 4 * (2 * D * Q + P * T + 2 * T + Q + I + E * T + Q + E * Q) + 16 * T + 2 * P * (I // 16)
+
+
+def tile_attend_maplace_pagewinners_rowchanges_kernel(
+    tc, query, query2, keys_words, keys_scales, xmark, ymark, lam, slot_factor, vals, memq, offs, out
+):
+    nc = tc.nc
+    with ExitStack() as ctx:
+        keep = ctx.enter_context(tc.tile_pool(name="keep", bufs=1))
+        pool = ctx.enter_context(tc.tile_pool(name="pool", bufs=1))
+        psum = ctx.enter_context(tc.psum_pool(name="psum", bufs=1))
+
+        def bank(tag, name):
+            return psum.tile([P, BANK], F32, tag=tag, name=name)
+
+        offsets = keep.tile([P, I // 16], U16, name="offsets")
+        nc.sync.dma_start(offsets[:], offs)
+
+        q_raw = [keep.tile([P, PACK, Q], F32, name="q_raw%d" % s) for s in range(2)]
+        kw_pool = pool.tile([P, T], U32, tag="w2", name="kw_pool")
+        ks_pool = pool.tile([P, T], U8, tag="w1", name="ks_pool")
+        x_pool = pool.tile([P, T], F32, tag="w0", name="x_pool")
+        y_pool = pool.tile([P, T], F32, tag="w3", name="y_pool")
+        nc.sync.dma_start(q_raw[0][:], query.rearrange("(p j) q -> p j q", j=PACK))
+        nc.sync.dma_start(kw_pool[:].bitcast(I32), keys_words[0].rearrange("p n t -> p (n t)").bitcast(I32))
+        nc.sync.dma_start(q_raw[1][:], query2.rearrange("(p j) q -> p j q", j=PACK))
+
+        ident = keep.tile([P, P], F32, name="ident")
+        make_identity(nc, ident[:])
+        lam_col = keep.tile([P, QT], F32, name="lam_col")
+        os_col = keep.tile([P, IT], F32, name="os_col")
+        mem_col = keep.tile([P, QT], F32, name="mem_col")
+        with nc.allow_non_contiguous_dma(reason="one value a partition"):
+            nc.gpsimd.dma_start(lam_col[:], lam.rearrange("(c p) o -> p (c o)", p=P))
+        nc.gpsimd.dma_start(os_col[:], slot_factor.rearrange("o (p c) -> p (o c)", c=IT))
+        nc.gpsimd.dma_start(mem_col[:], memq.rearrange("o (p c) -> p (o c)", c=QT))
+
+        nc.vector.memset(x_pool[:].bitcast(I32), 0)
+        nc.scalar.dma_start(x_pool[0:1, :], xmark[0:1, :])
+        nc.vector.memset(ks_pool[:].bitcast(I32), 0)
+        for quad in range(4):
+            nc.scalar.dma_start(
+                ks_pool[32 * quad : 32 * quad + 4, :].bitcast(I32),
+                keys_scales[0, 4 * quad : 4 * quad + 4, :].bitcast(I32),
+            )
+        nc.vector.memset(y_pool[:].bitcast(I32), 0)
+        nc.sync.dma_start(y_pool[0:1, :], ymark[0:1, :])
+        carried = keep.tile([P, ET, Q], F32, name="carried")
+        nc.gpsimd.memset(carried[:, :, 0], 0.0)
+
+        lam_neg = keep.tile([P, 2, QT], F32, name="lam_neg")
+        nc.gpsimd.tensor_scalar(lam_neg[:, 0, :], lam_col[:], -1.0, 0.0, ALU.mult, ALU.add)
+        nc.gpsimd.tensor_scalar(lam_neg[:, 1, :], lam_col[:], -2.0, 0.0, ALU.mult, ALU.add)
+
+        ks = keep.tile([P, I], U8, name="ks", align_bytes=64)
+
+        q_grp = [keep.tile([P, Q, PACK], BF16, name="q_grp%d" % s, align_bytes=64) for s in range(2)]
+        q_codes = [keep.tile([P, Q], U32, name="q_codes%d" % s, align_bytes=64) for s in range(2)]
+        q_scales = [keep.tile([P, Q], U8, name="q_scales%d" % s, align_bytes=64) for s in range(2)]
+
+        def interleave_query(s):
+            nc.scalar.activation(
+                q_grp[s][:].rearrange("p (c i) t -> p c t i", i=4),
+                q_raw[s][:].rearrange("p t (c i) -> p c t i", i=4),
+                ACT.Copy,
+            )
+
+        def quantize_query(s):
+            nc.vector.quantize_mx(
+                out=q_codes[s][:].bitcast(FP8X4), scales=q_scales[s][:], in_=q_grp[s][:].rearrange("p q t -> p (q t)")
+            )
+
+        marks = [keep.tile([P, IT], F32, name="marks%d" % s) for s in range(2)]
+
+        def gather_mark(s, window):
+            row = keep.tile([P, I], F32, name="mark_row%d" % s)
+            nc.vector.tensor_copy(row[:], window[:].indirect(offsets[:]))
+            turned = bank("d%d" % s, "mark_bank%d" % s)
+            for r in range(IT):
+                nc.tensor.transpose(turned[:, r * P : (r + 1) * P], row[:, r * P : (r + 1) * P], ident[:])
+            nc.scalar.copy(marks[s][:], turned[:].rearrange("p (r m) -> p r m", m=P)[:, :, 0])
+
+        interleave_query(0)
+        gather_mark(0, x_pool)
+        nc.vector.tensor_copy(ks[:], ks_pool[:].indirect(offsets[:]))
+        quantize_query(0)
+        kw = keep.tile([P, I], U32, name="kw", align_bytes=64)
+        nc.vector.tensor_copy(kw[:], kw_pool[:].indirect(offsets[:]))
+        interleave_query(1)
+
+        v_pool = []
+        for b in range(ET):
+            window = pool.tile([P, T], F32, tag="w%d" % b, name="v_pool%d" % b)
+            v_pool.append(window)
+
+        sq = [[keep.tile([P, Q], F32, name="sq%d_%d" % (s, r)) for r in range(IT)] for s in range(2)]
+
+        def scores(s):
+            banks = [bank("s%d" % (2 * s + h), "score%d_%d" % (s, h)) for h in range(2)]
+            for r in range(IT):
+                nc.tensor.matmul_mx(
+                    out=banks[r // 2][:, (r % 2) * Q : (r % 2 + 1) * Q],
+                    lhsT=kw[:, r * P : (r + 1) * P].bitcast(FP8X4),
+                    lhsT_scale=ks[:, r * P : (r + 1) * P],
+                    rhs=q_codes[s][:].bitcast(FP8X4),
+                    rhs_scale=q_scales[s][:],
+                    start=True,
+                    stop=True,
+                )
+            for r in range(IT):
+                nc.scalar.activation(
+                    sq[s][r][:],
+                    banks[r // 2][:, (r % 2) * Q : (r % 2 + 1) * Q],
+                    ACT.Square,
+                    bias=marks[s][:, r : r + 1],
+                    scale=-1.0,
+                )
+
+        nc.sync.dma_start(v_pool[0][:], vals[0:P, :])
+        nc.sync.dma_start(v_pool[1][:], vals[P : 2 * P, :])
+        nc.sync.dma_start(v_pool[2][:], vals[2 * P : 3 * P, :])
+        scores(0)
+        gather_mark(1, y_pool)
+        quantize_query(1)
+        nc.sync.dma_start(v_pool[3][:], vals[3 * P : 4 * P, :])
+        scores(1)
+        os_bank = bank("s1", "os_bank")
+        for c in range(IT):
+            nc.tensor.transpose(os_bank[:, c * P : (c + 1) * P], os_col[:, c : c + 1].to_broadcast([P, P]), ident[:])
+
+
+        dist = [bank("d%d" % t, "dist%d" % t) for t in range(QT)]
+        for s in range(2):
+            for r in range(IT):
+                for t in range(QT):
+                    nc.tensor.matmul(
+                        dist[t][:, r * P : (r + 1) * P],
+                        sq[s][r][:, t * P : (t + 1) * P],
+                        ident[:],
+                        start=(s == 0 and r == 0),
+                        stop=(s == 1 and r == IT - 1),
+                        is_transpose=True,
+                    )
+
+        v_codes = [keep.tile([P, P], U32, name="v_codes%d" % b, align_bytes=64) for b in range(ET)]
+        v_scales = [keep.tile([P, P], U8, name="v_scales%d" % b, align_bytes=64) for b in range(ET)]
+        v_grp = [keep.tile([P, P, PACK], BF16, name="v_grp%d" % b, align_bytes=64) for b in range(ET)]
+
+        def turn_words(rows, turned, grouped):
+            words = rows.bitcast(F32)
+            for u in range(2):
+                nc.tensor.transpose(turned[:, u * P : (u + 1) * P], words[:, u : 2 * P : 2], ident[:])
+            nc.scalar.copy(
+                grouped.rearrange("p c t -> p (c t)").bitcast(F32).rearrange("p (c u) -> p c u", u=2),
+                turned[:, 0 : 2 * P].rearrange("p (u c) -> p c u", u=2),
+            )
+
+        def gather_values(b, tag):
+            picked = keep.tile([P, I], BF16, name="picked%d" % b)
+            nc.vector.tensor_copy(picked[:], v_pool[b][:].indirect(offsets[:]))
+            turn_words(picked[:], bank(tag, "v_bank%d" % b), v_grp[b][:])
+
+        def quantize_values(b):
+            nc.vector.quantize_mx(
+                out=v_codes[b][:].bitcast(FP8X4), scales=v_scales[b][:], in_=v_grp[b][:].rearrange("p c t -> p (c t)")
+            )
+
+        gather_values(0, "t")
+        p1 = [keep.tile([P, I], F32, name="p1_%d" % t) for t in range(QT)]
+        p2 = [keep.tile([P, I], F32, name="p2_%d" % t) for t in range(QT)]
+        for t in range(QT):
+            nc.scalar.activation(p1[t][:], dist[t][:], ACT.Exp, scale=lam_neg[:, 0, t : t + 1])
+        for t in range(QT):
+            nc.scalar.activation(p2[t][:], dist[t][:], ACT.Exp, scale=lam_neg[:, 1, t : t + 1])
+        quantize_values(0)
+        gather_values(1, "u")
+
+        pg = keep.tile([P, QT, G], F32, name="pg")
+        for t in range(QT):
+            nc.vector.tensor_reduce(pg[:, t, :], p1[t][:].rearrange("p (g j) -> p g j", j=RUN), AXIS.X, ALU.add)
+        inv_root = keep.tile([P, QT, G], F32, name="inv_root")
+        nc.scalar.activation(inv_root[:], pg[:], ACT.Abs_reciprocal_sqrt)
+        inv_pg = keep.tile([P, QT, G], F32, name="inv_pg")
+        nc.scalar.activation(inv_pg[:], inv_root[:], ACT.Square)
+        mem_bank = bank("d0", "mem_bank")
+        for c in range(QT):
+            nc.tensor.transpose(mem_bank[:, c * P : (c + 1) * P], mem_col[:, c : c + 1].to_broadcast([P, P]), ident[:])
+        mem_row = keep.tile([P, Q], F32, name="mem_row")
+        nc.scalar.copy(
+            mem_row[:].rearrange("m (p c) -> m p c", c=QT),
+            mem_bank[:, 0:Q].rearrange("m (c p) -> m p c", c=QT),
+        )
+        p2os = [keep.tile([P, I], F32, name="p2os%d" % t) for t in range(QT)]
+        for t in range(QT):
+            nc.vector.tensor_tensor(
+                p2os[t][:].rearrange("m (p c) -> m p c", c=IT),
+                p2[t][:].rearrange("m (p c) -> m p c", c=IT),
+                os_bank[:].rearrange("m (c p) -> m p c", c=IT),
+                ALU.mult,
+            )
+        quantize_values(1)
+        gather_values(2, "t")
+
+        root = keep.tile([P, QT, G], F32, name="root")
+        root_sum = keep.tile([P, QT], F32, name="root_sum")
+        for t in range(QT):
+            nc.vector.scalar_tensor_tensor(
+                root[:, t, :], pg[:, t, :], 1.0, inv_root[:, t, :], ALU.mult, ALU.mult, accum_out=root_sum[:, t : t + 1]
+            )
+        factor = keep.tile([P, QT, G], F32, name="factor")
+        nc.vector.tensor_tensor(factor[:], inv_pg[:], inv_root[:], ALU.mult)
+        inv_sum = keep.tile([P, QT], F32, name="inv_sum")
+        nc.vector.reciprocal(inv_sum[:], root_sum[:])
+
+        w_grp = keep.tile([P, Q, PACK], BF16, name="w_grp", align_bytes=64)
+        for t in range(QT):
+            weights = keep.tile([P, I], BF16, name="weights%d" % t)
+            nc.vector.scalar_tensor_tensor(
+                weights[:].rearrange("p (g j) -> p g j", j=RUN),
+                p2os[t][:].rearrange("p (g j) -> p g j", j=RUN),
+                inv_sum[:, t : t + 1],
+                factor[:, t, :].unsqueeze(2).to_broadcast([P, G, RUN]),
+                ALU.mult,
+                ALU.mult,
+            )
+            turn_words(weights[:], bank("s%d" % (2 + t), "w_bank%d" % t), w_grp[:, t * P : (t + 1) * P, :])
+        quantize_values(2)
+        gather_values(3, "u")
+        w_codes = keep.tile([P, Q], U32, name="w_codes", align_bytes=64)
+        w_scales = keep.tile([P, Q], U8, name="w_scales", align_bytes=64)
+        nc.vector.quantize_mx(
+            out=w_codes[:].bitcast(FP8X4), scales=w_scales[:], in_=w_grp[:].rearrange("p c t -> p (c t)")
+        )
+        quantize_values(3)
+
+        for b, tag in enumerate(("d1", "s0", "d0", "s1")):
+            acc = bank(tag, "acc%d" % b)
+            nc.tensor.matmul_mx(
+                out=acc[:, 0:Q],
+                lhsT=v_codes[b][:].bitcast(FP8X4),
+                lhsT_scale=v_scales[b][:],
+                rhs=w_codes[:].bitcast(FP8X4),
+                rhs_scale=w_scales[:],
+                start=True,
+                stop=True,
+            )
+            nc.vector.tensor_tensor(carried[:, b, 1:Q], acc[:, 0 : Q - 1], mem_row[:, 1:Q], ALU.mult)
+            result = keep.tile([P, Q], F32, name="result%d" % b)
+            nc.vector.tensor_tensor(result[:], acc[:, 0:Q], carried[:, b, :], ALU.subtract)
+            nc.sync.dma_start(out[b * P : (b + 1) * P, :], result[:])

@@ -22,6 +22,7 @@ BANK = 512
 QT = Q // P
 IT = I // P
 ET = E // P
+HALF = ET // 2
 
 FLOPS = 2 * 2 * D * Q * I + 2 * I * E * Q
 BYTES = 4 * (2 * D * Q + P * T + 2 * T + Q + I + E * T + Q + E * Q) + 16 * T + 2 * P * (I // 16)
@@ -42,45 +43,33 @@ def tile_attend_maplace_pagewinners_rowchanges_kernel(
         offsets = keep.tile([P, I // 16], U16, name="offsets")
         nc.sync.dma_start(offsets[:], offs)
 
-        q_raw = [keep.tile([P, PACK, Q], F32, name="q_raw%d" % s) for s in range(2)]
-        kw_pool = pool.tile([P, T], U32, tag="w2", name="kw_pool")
-        ks_pool = pool.tile([P, T], U8, tag="w1", name="ks_pool")
-        x_pool = pool.tile([P, T], F32, tag="w0", name="x_pool")
-        y_pool = pool.tile([P, T], F32, tag="w3", name="y_pool")
+        q_raw = [pool.tile([P, PACK, Q], F32, tag=tag, name="q_raw%d" % s) for s, tag in enumerate(("w1", "wq"))]
+        kw_pool = pool.tile([P, T], U32, tag="w3", name="kw_pool")
+        ks_pool = pool.tile([P, T], U8, tag="w0", name="ks_pool")
+        x_pool = pool.tile([P, T], F32, tag="wx", name="x_pool", align_bytes=64)
+        y_pool = pool.tile([P, T], F32, tag="w2", name="y_pool")
+        nc.gpsimd.memset(ks_pool[:].bitcast(I32), 0)
         nc.sync.dma_start(q_raw[0][:], query.rearrange("(p j) q -> p j q", j=PACK))
-        nc.sync.dma_start(kw_pool[:].bitcast(I32), keys_words[0].rearrange("p n t -> p (n t)").bitcast(I32))
-        nc.sync.dma_start(q_raw[1][:], query2.rearrange("(p j) q -> p j q", j=PACK))
-
-        ident = keep.tile([P, P], F32, name="ident")
-        make_identity(nc, ident[:])
-        lam_col = keep.tile([P, QT], F32, name="lam_col")
-        os_col = keep.tile([P, IT], F32, name="os_col")
-        mem_col = keep.tile([P, QT], F32, name="mem_col")
-        with nc.allow_non_contiguous_dma(reason="one value a partition"):
-            nc.gpsimd.dma_start(lam_col[:], lam.rearrange("(c p) o -> p (c o)", p=P))
-        nc.gpsimd.dma_start(os_col[:], slot_factor.rearrange("o (p c) -> p (o c)", c=IT))
-        nc.gpsimd.dma_start(mem_col[:], memq.rearrange("o (p c) -> p (o c)", c=QT))
-
-        nc.vector.memset(x_pool[:].bitcast(I32), 0)
-        nc.scalar.dma_start(x_pool[0:1, :], xmark[0:1, :])
-        nc.vector.memset(ks_pool[:].bitcast(I32), 0)
         for quad in range(4):
-            nc.scalar.dma_start(
+            nc.sync.dma_start(
                 ks_pool[32 * quad : 32 * quad + 4, :].bitcast(I32),
                 keys_scales[0, 4 * quad : 4 * quad + 4, :].bitcast(I32),
             )
+        nc.sync.dma_start(kw_pool[:].bitcast(I32), keys_words[0].rearrange("p n t -> p (n t)").bitcast(I32))
+        nc.sync.dma_start(q_raw[1][:], query2.rearrange("(p j) q -> p j q", j=PACK))
+        nc.vector.memset(x_pool[:].bitcast(I32), 0)
+        nc.scalar.dma_start(x_pool[0:1, :], xmark[0:1, :])
         nc.vector.memset(y_pool[:].bitcast(I32), 0)
-        nc.sync.dma_start(y_pool[0:1, :], ymark[0:1, :])
+        nc.scalar.dma_start(y_pool[0:1, :], ymark[0:1, :])
+
+        ident = keep.tile([P, P], F32, name="ident")
+        make_identity(nc, ident[:])
         carried = keep.tile([P, ET, Q], F32, name="carried")
         nc.gpsimd.memset(carried[:, :, 0], 0.0)
 
-        lam_neg = keep.tile([P, 2, QT], F32, name="lam_neg")
-        nc.gpsimd.tensor_scalar(lam_neg[:, 0, :], lam_col[:], -1.0, 0.0, ALU.mult, ALU.add)
-        nc.gpsimd.tensor_scalar(lam_neg[:, 1, :], lam_col[:], -2.0, 0.0, ALU.mult, ALU.add)
-
         ks = keep.tile([P, I], U8, name="ks", align_bytes=64)
 
-        q_grp = [keep.tile([P, Q, PACK], BF16, name="q_grp%d" % s, align_bytes=64) for s in range(2)]
+        q_grp = [pool.tile([P, Q, PACK], BF16, tag="grp%d" % s, name="q_grp%d" % s, align_bytes=64) for s in range(2)]
         q_codes = [keep.tile([P, Q], U32, name="q_codes%d" % s, align_bytes=64) for s in range(2)]
         q_scales = [keep.tile([P, Q], U8, name="q_scales%d" % s, align_bytes=64) for s in range(2)]
 
@@ -98,25 +87,32 @@ def tile_attend_maplace_pagewinners_rowchanges_kernel(
 
         marks = [keep.tile([P, IT], F32, name="marks%d" % s) for s in range(2)]
 
-        def gather_mark(s, window):
-            row = keep.tile([P, I], F32, name="mark_row%d" % s)
+        def gather_mark(s, window, row_tag, tag):
+            row = pool.tile([P, I], F32, tag=row_tag, name="mark_row%d" % s)
             nc.vector.tensor_copy(row[:], window[:].indirect(offsets[:]))
-            turned = bank("d%d" % s, "mark_bank%d" % s)
+            turned = bank(tag, "mark_bank%d" % s)
             for r in range(IT):
                 nc.tensor.transpose(turned[:, r * P : (r + 1) * P], row[:, r * P : (r + 1) * P], ident[:])
             nc.scalar.copy(marks[s][:], turned[:].rearrange("p (r m) -> p r m", m=P)[:, :, 0])
 
         interleave_query(0)
-        gather_mark(0, x_pool)
         nc.vector.tensor_copy(ks[:], ks_pool[:].indirect(offsets[:]))
+        gather_mark(0, x_pool, "xrow", "d0")
         quantize_query(0)
-        kw = keep.tile([P, I], U32, name="kw", align_bytes=64)
+        os_col = pool.tile([P, IT], F32, tag="grp0", name="os_col", align_bytes=64)
+        nc.scalar.dma_start(os_col[:], slot_factor.rearrange("o (p c) -> p (o c)", c=IT))
+        lam_col = pool.tile([P, QT], F32, tag="xrow", name="lam_col")
+        with nc.allow_non_contiguous_dma(reason="one value a partition"):
+            nc.scalar.dma_start(lam_col[:], lam.rearrange("(c p) o -> p (c o)", p=P))
+        kw = pool.tile([P, I], U32, tag="wx", name="kw", align_bytes=64)
         nc.vector.tensor_copy(kw[:], kw_pool[:].indirect(offsets[:]))
         interleave_query(1)
 
         v_pool = []
-        for b in range(ET):
+
+        def load_values(b):
             window = pool.tile([P, T], F32, tag="w%d" % b, name="v_pool%d" % b)
+            nc.sync.dma_start(window[:], vals[b * P : (b + 1) * P, :])
             v_pool.append(window)
 
         sq = [[keep.tile([P, Q], F32, name="sq%d_%d" % (s, r)) for r in range(IT)] for s in range(2)]
@@ -142,19 +138,19 @@ def tile_attend_maplace_pagewinners_rowchanges_kernel(
                     scale=-1.0,
                 )
 
-        nc.sync.dma_start(v_pool[0][:], vals[0:P, :])
-        nc.sync.dma_start(v_pool[1][:], vals[P : 2 * P, :])
-        nc.sync.dma_start(v_pool[2][:], vals[2 * P : 3 * P, :])
+        load_values(0)
+        load_values(1)
         scores(0)
-        gather_mark(1, y_pool)
+        gather_mark(1, y_pool, "w3", "u")
         quantize_query(1)
-        nc.sync.dma_start(v_pool[3][:], vals[3 * P : 4 * P, :])
+        mem_col = pool.tile([P, QT], F32, tag="grp1", name="mem_col", align_bytes=64)
+        nc.sync.dma_start(mem_col[:], memq.rearrange("o (p c) -> p (o c)", c=QT))
+        lam_neg = keep.tile([P, 2, QT], F32, name="lam_neg")
+        nc.vector.tensor_scalar(lam_neg[:, 0, :], lam_col[:], -1.0, None, ALU.mult)
+        nc.vector.tensor_scalar(lam_neg[:, 1, :], lam_col[:], -2.0, None, ALU.mult)
+        load_values(2)
+        load_values(3)
         scores(1)
-        os_bank = bank("s1", "os_bank")
-        for c in range(IT):
-            nc.tensor.transpose(os_bank[:, c * P : (c + 1) * P], os_col[:, c : c + 1].to_broadcast([P, P]), ident[:])
-
-
         dist = [bank("d%d" % t, "dist%d" % t) for t in range(QT)]
         for s in range(2):
             for r in range(IT):
@@ -168,47 +164,74 @@ def tile_attend_maplace_pagewinners_rowchanges_kernel(
                         is_transpose=True,
                     )
 
-        v_codes = [keep.tile([P, P], U32, name="v_codes%d" % b, align_bytes=64) for b in range(ET)]
-        v_scales = [keep.tile([P, P], U8, name="v_scales%d" % b, align_bytes=64) for b in range(ET)]
-        v_grp = [keep.tile([P, P, PACK], BF16, name="v_grp%d" % b, align_bytes=64) for b in range(ET)]
+        os_bank = bank("s3", "os_bank")
+        for c in range(IT):
+            nc.tensor.transpose(os_bank[:, c * P : (c + 1) * P], os_col[:, c : c + 1].to_broadcast([P, P]), ident[:])
 
-        def turn_words(rows, turned, grouped):
-            words = rows.bitcast(F32)
-            for u in range(2):
-                nc.tensor.transpose(turned[:, u * P : (u + 1) * P], words[:, u : 2 * P : 2], ident[:])
+
+        def turn_words(tiles, turned, grouped):
+            for n, rows in enumerate(tiles):
+                words = rows[:].bitcast(F32)
+                for u in range(2):
+                    cols = slice((2 * n + u) * P, (2 * n + u + 1) * P)
+                    nc.tensor.transpose(turned[:, cols], words[:, u : 2 * P : 2], ident[:])
             nc.scalar.copy(
-                grouped.rearrange("p c t -> p (c t)").bitcast(F32).rearrange("p (c u) -> p c u", u=2),
-                turned[:, 0 : 2 * P].rearrange("p (u c) -> p c u", u=2),
+                grouped.bitcast(F32).rearrange("p (n c u) -> p n c u", u=2, c=P),
+                turned[:, 0 : 2 * P * len(tiles)].rearrange("p (n u c) -> p n c u", u=2, c=P),
             )
 
-        def gather_values(b, tag):
-            picked = keep.tile([P, I], BF16, name="picked%d" % b)
-            nc.vector.tensor_copy(picked[:], v_pool[b][:].indirect(offsets[:]))
-            turn_words(picked[:], bank(tag, "v_bank%d" % b), v_grp[b][:])
+        picked = [keep.tile([P, I], BF16, name="picked%d" % b) for b in range(ET)]
+        for b in range(ET):
+            nc.vector.tensor_copy(picked[b][:], v_pool[b][:].indirect(offsets[:]))
 
-        def quantize_values(b):
-            nc.vector.quantize_mx(
-                out=v_codes[b][:].bitcast(FP8X4), scales=v_scales[b][:], in_=v_grp[b][:].rearrange("p c t -> p (c t)")
-            )
-
-        gather_values(0, "t")
-        p1 = [keep.tile([P, I], F32, name="p1_%d" % t) for t in range(QT)]
-        p2 = [keep.tile([P, I], F32, name="p2_%d" % t) for t in range(QT)]
+        p1 = pool.tile([P, RUN, QT * G], F32, tag="p1", name="p1", align_bytes=64)
+        p2 = [pool.tile([P, I], F32, tag="p2_%d" % t, name="p2_%d" % t) for t in range(QT)]
         for t in range(QT):
-            nc.scalar.activation(p1[t][:], dist[t][:], ACT.Exp, scale=lam_neg[:, 0, t : t + 1])
+            nc.scalar.activation(
+                p1[:, :, t * G : (t + 1) * G],
+                dist[t][:].rearrange("p (g j) -> p j g", j=RUN),
+                ACT.Exp,
+                scale=lam_neg[:, 0, t : t + 1],
+            )
         for t in range(QT):
             nc.scalar.activation(p2[t][:], dist[t][:], ACT.Exp, scale=lam_neg[:, 1, t : t + 1])
-        quantize_values(0)
-        gather_values(1, "u")
 
-        pg = keep.tile([P, QT, G], F32, name="pg")
-        for t in range(QT):
-            nc.vector.tensor_reduce(pg[:, t, :], p1[t][:].rearrange("p (g j) -> p g j", j=RUN), AXIS.X, ALU.add)
+        sums_turned = bank("s0", "sums_turned")
+        for j in range(RUN):
+            nc.tensor.matmul(
+                sums_turned[:, 0:P], p1[:, j, :], ident[:], start=(j == 0), stop=(j == RUN - 1), is_transpose=True
+            )
+        sums_staged = pool.tile([P, P], F32, tag="staged", name="sums_staged", align_bytes=64)
+        nc.vector.tensor_copy(sums_staged[:], sums_turned[:, 0:P])
+        pg_bank = bank("s1", "pg_bank")
+        nc.tensor.transpose(pg_bank[:, 0:P], sums_staged[:], ident[:])
+        pg = pg_bank[:, 0:P].rearrange("p (t g) -> p t g", g=G)
         inv_root = keep.tile([P, QT, G], F32, name="inv_root")
-        nc.scalar.activation(inv_root[:], pg[:], ACT.Abs_reciprocal_sqrt)
+        nc.scalar.activation(inv_root[:], pg, ACT.Abs_reciprocal_sqrt)
         inv_pg = keep.tile([P, QT, G], F32, name="inv_pg")
         nc.scalar.activation(inv_pg[:], inv_root[:], ACT.Square)
-        mem_bank = bank("d0", "mem_bank")
+        v_grp = pool.tile([P, E * PACK], BF16, tag="staged", name="v_grp", align_bytes=64)
+        for h, tag in enumerate(("s0", "d1")):
+            turn_words(picked[2 * h : 2 * h + 2], bank(tag, "v_bank%d" % h), v_grp[:, h * 2 * I : (h + 1) * 2 * I])
+        p2os = pool.tile([P, QT, I], F32, tag="p1", name="p2os", align_bytes=64)
+        for t in range(QT):
+            nc.vector.tensor_tensor(
+                p2os[:, t, :].rearrange("m (p c) -> m p c", c=IT),
+                p2[t][:].rearrange("m (p c) -> m p c", c=IT),
+                os_bank[:].rearrange("m (c p) -> m p c", c=IT),
+                ALU.mult,
+            )
+
+        root = keep.tile([P, QT, G], F32, name="root")
+        root_sum = keep.tile([P, QT], F32, name="root_sum")
+        nc.vector.tensor_tensor(root[:], pg, inv_root[:], ALU.mult)
+        factor = keep.tile([P, QT, G], F32, name="factor")
+        nc.vector.tensor_tensor(factor[:], inv_pg[:], inv_root[:], ALU.mult)
+        nc.vector.tensor_reduce(root_sum[:], root[:], AXIS.X, ALU.add)
+        inv_sum = keep.tile([P, QT], F32, name="inv_sum")
+        nc.vector.reciprocal(inv_sum[:], root_sum[:])
+
+        mem_bank = bank("s1", "mem_bank")
         for c in range(QT):
             nc.tensor.transpose(mem_bank[:, c * P : (c + 1) * P], mem_col[:, c : c + 1].to_broadcast([P, P]), ident[:])
         mem_row = keep.tile([P, Q], F32, name="mem_row")
@@ -216,61 +239,53 @@ def tile_attend_maplace_pagewinners_rowchanges_kernel(
             mem_row[:].rearrange("m (p c) -> m p c", c=QT),
             mem_bank[:, 0:Q].rearrange("m (c p) -> m p c", c=QT),
         )
-        p2os = [keep.tile([P, I], F32, name="p2os%d" % t) for t in range(QT)]
-        for t in range(QT):
-            nc.vector.tensor_tensor(
-                p2os[t][:].rearrange("m (p c) -> m p c", c=IT),
-                p2[t][:].rearrange("m (p c) -> m p c", c=IT),
-                os_bank[:].rearrange("m (c p) -> m p c", c=IT),
-                ALU.mult,
-            )
-        quantize_values(1)
-        gather_values(2, "t")
-
-        root = keep.tile([P, QT, G], F32, name="root")
-        root_sum = keep.tile([P, QT], F32, name="root_sum")
-        for t in range(QT):
-            nc.vector.scalar_tensor_tensor(
-                root[:, t, :], pg[:, t, :], 1.0, inv_root[:, t, :], ALU.mult, ALU.mult, accum_out=root_sum[:, t : t + 1]
-            )
-        factor = keep.tile([P, QT, G], F32, name="factor")
-        nc.vector.tensor_tensor(factor[:], inv_pg[:], inv_root[:], ALU.mult)
-        inv_sum = keep.tile([P, QT], F32, name="inv_sum")
-        nc.vector.reciprocal(inv_sum[:], root_sum[:])
-
-        w_grp = keep.tile([P, Q, PACK], BF16, name="w_grp", align_bytes=64)
+        w_grp = [keep.tile([P, P * PACK], BF16, name="w_grp%d" % t, align_bytes=64) for t in range(QT)]
         for t in range(QT):
             weights = keep.tile([P, I], BF16, name="weights%d" % t)
             nc.vector.scalar_tensor_tensor(
                 weights[:].rearrange("p (g j) -> p g j", j=RUN),
-                p2os[t][:].rearrange("p (g j) -> p g j", j=RUN),
+                p2os[:, t, :].rearrange("p (g j) -> p g j", j=RUN),
                 inv_sum[:, t : t + 1],
                 factor[:, t, :].unsqueeze(2).to_broadcast([P, G, RUN]),
                 ALU.mult,
                 ALU.mult,
             )
-            turn_words(weights[:], bank("s%d" % (2 + t), "w_bank%d" % t), w_grp[:, t * P : (t + 1) * P, :])
-        quantize_values(2)
-        gather_values(3, "u")
-        w_codes = keep.tile([P, Q], U32, name="w_codes", align_bytes=64)
-        w_scales = keep.tile([P, Q], U8, name="w_scales", align_bytes=64)
-        nc.vector.quantize_mx(
-            out=w_codes[:].bitcast(FP8X4), scales=w_scales[:], in_=w_grp[:].rearrange("p c t -> p (c t)")
-        )
-        quantize_values(3)
-
-        for b, tag in enumerate(("d1", "s0", "d0", "s1")):
-            acc = bank(tag, "acc%d" % b)
-            nc.tensor.matmul_mx(
-                out=acc[:, 0:Q],
-                lhsT=v_codes[b][:].bitcast(FP8X4),
-                lhsT_scale=v_scales[b][:],
-                rhs=w_codes[:].bitcast(FP8X4),
-                rhs_scale=w_scales[:],
-                start=True,
-                stop=True,
+            turn_words([weights], bank("s%d" % (2 + t), "w_bank%d" % t), w_grp[t][:])
+        v_codes = pool.tile([P, E], U32, tag="p1", name="v_codes", align_bytes=64)
+        v_scales = keep.tile([P, E], U8, name="v_scales", align_bytes=64)
+        nc.vector.quantize_mx(out=v_codes[:].bitcast(FP8X4), scales=v_scales[:], in_=v_grp[:])
+        result = keep.tile([P, ET, Q], F32, name="result")
+        for t in range(QT):
+            w_codes = keep.tile([P, P], U32, name="w_codes%d" % t, align_bytes=64)
+            w_scales = keep.tile([P, P], U8, name="w_scales%d" % t, align_bytes=64)
+            nc.vector.quantize_mx(
+                out=w_codes[:].bitcast(FP8X4), scales=w_scales[:], in_=w_grp[t][:]
             )
-            nc.vector.tensor_tensor(carried[:, b, 1:Q], acc[:, 0 : Q - 1], mem_row[:, 1:Q], ALU.mult)
-            result = keep.tile([P, Q], F32, name="result%d" % b)
-            nc.vector.tensor_tensor(result[:], acc[:, 0:Q], carried[:, b, :], ALU.subtract)
-            nc.sync.dma_start(out[b * P : (b + 1) * P, :], result[:])
+            halves = [slice(h * HALF, (h + 1) * HALF) for h in range(2)]
+            sums = []
+            for half, tag in zip(halves, (("t", "u"), ("d0", "s0"))[t]):
+                acc = bank(tag, "acc%d_%d" % (t, half.start))
+                for n, b in enumerate(range(half.start, half.stop)):
+                    nc.tensor.matmul_mx(
+                        out=acc[:, n * P : (n + 1) * P],
+                        lhsT=v_codes[:, b * P : (b + 1) * P].bitcast(FP8X4),
+                        lhsT_scale=v_scales[:, b * P : (b + 1) * P],
+                        rhs=w_codes[:].bitcast(FP8X4),
+                        rhs_scale=w_scales[:],
+                        start=True,
+                        stop=True,
+                    )
+                sums.append(acc[:, 0 : HALF * P].rearrange("p (b q) -> p b q", b=HALF))
+            first = t * P + 1
+            count = min(P, Q - first)
+            for half, part in zip(halves, sums):
+                nc.vector.tensor_tensor(
+                    carried[:, half, first : first + count],
+                    part[:, :, 0:count],
+                    mem_row[:, first : first + count].unsqueeze(1).to_broadcast([P, HALF, count]),
+                    ALU.mult,
+                )
+            for half, part, queue in zip(halves, sums, (nc.sync, nc.scalar if t == QT - 1 else nc.sync)):
+                cols = slice(t * P, (t + 1) * P)
+                nc.vector.tensor_tensor(result[:, half, cols], part, carried[:, half, cols], ALU.subtract)
+                queue.dma_start(out.rearrange("(b p) q -> p b q", p=P)[:, half, cols], result[:, half, cols])

from contextlib import ExitStack

import concourse.mybir as mybir
from concourse.masks import make_identity

F32 = mybir.dt.float32
BF16 = mybir.dt.bfloat16
I32 = mybir.dt.int32
U32 = mybir.dt.uint32
U16 = mybir.dt.uint16
U8 = mybir.dt.uint8
FP8X4 = mybir.dt.float8_e4m3fn_x4
ACT = mybir.ActivationFunctionType
ALU = mybir.AluOpType
AXIS = mybir.AxisListType

D, T, I, Q, E, G = 512, 2048, 512, 256, 512, 64
P = 128
PACK = 4
RUN = I // G
BANK = 512
QT = Q // P
IT = I // P
ET = E // P
HALF = ET // 2

FLOPS = 2 * 2 * D * Q * I + 2 * I * E * Q
BYTES = 4 * (2 * D * Q + P * T + 2 * T + Q + I + E * T + Q + E * Q) + 16 * T + 2 * P * (I // 16)


def tile_attend_maplace_pagewinners_rowchanges_kernel(
    tc, query, query2, keys_words, keys_scales, xmark, ymark, lam, slot_factor, vals, memq, offs, out
):
    nc = tc.nc
    with ExitStack() as ctx:
        keep = ctx.enter_context(tc.tile_pool(name="keep", bufs=1))
        pool = ctx.enter_context(tc.tile_pool(name="pool", bufs=1))
        psum = ctx.enter_context(tc.psum_pool(name="psum", bufs=1))

        def bank(tag, name):
            return psum.tile([P, BANK], F32, tag=tag, name=name)

        offsets = keep.tile([P, I // 16], U16, name="offsets")
        nc.sync.dma_start(offsets[:], offs)

        q_raw = [pool.tile([P, PACK, Q], F32, tag=tag, name="q_raw%d" % s) for s, tag in enumerate(("w1", "wq"))]
        kw_pool = pool.tile([P, T], U32, tag="w3", name="kw_pool")
        ks_pool = pool.tile([P, T], U8, tag="w0", name="ks_pool")
        x_pool = pool.tile([P, T], F32, tag="wx", name="x_pool", align_bytes=64)
        y_pool = pool.tile([P, T], F32, tag="w2", name="y_pool")
        nc.gpsimd.memset(ks_pool[:].bitcast(I32), 0)
        nc.sync.dma_start(q_raw[0][:], query.rearrange("(p j) q -> p j q", j=PACK))
        for quad in range(4):
            nc.sync.dma_start(
                ks_pool[32 * quad : 32 * quad + 4, :].bitcast(I32),
                keys_scales[0, 4 * quad : 4 * quad + 4, :].bitcast(I32),
            )
        nc.sync.dma_start(kw_pool[:].bitcast(I32), keys_words[0].rearrange("p n t -> p (n t)").bitcast(I32))
        nc.sync.dma_start(q_raw[1][:], query2.rearrange("(p j) q -> p j q", j=PACK))
        nc.vector.memset(x_pool[:].bitcast(I32), 0)
        nc.scalar.dma_start(x_pool[0:1, :], xmark[0:1, :])
        nc.vector.memset(y_pool[:].bitcast(I32), 0)
        nc.scalar.dma_start(y_pool[0:1, :], ymark[0:1, :])

        ident = keep.tile([P, P], F32, name="ident")
        make_identity(nc, ident[:])
        carried = keep.tile([P, ET, Q], F32, name="carried")
        nc.gpsimd.memset(carried[:, :, 0], 0.0)

        ks = keep.tile([P, I], U8, name="ks", align_bytes=64)

        q_grp = [pool.tile([P, Q, PACK], BF16, tag="grp%d" % s, name="q_grp%d" % s, align_bytes=64) for s in range(2)]
        q_codes = [keep.tile([P, Q], U32, name="q_codes%d" % s, align_bytes=64) for s in range(2)]
        q_scales = [keep.tile([P, Q], U8, name="q_scales%d" % s, align_bytes=64) for s in range(2)]

        def interleave_query(s):
            nc.scalar.activation(
                q_grp[s][:].rearrange("p (c i) t -> p c t i", i=4),
                q_raw[s][:].rearrange("p t (c i) -> p c t i", i=4),
                ACT.Copy,
            )

        def quantize_query(s):
            nc.vector.quantize_mx(
                out=q_codes[s][:].bitcast(FP8X4), scales=q_scales[s][:], in_=q_grp[s][:].rearrange("p q t -> p (q t)")
            )

        marks = [keep.tile([P, IT], F32, name="marks%d" % s) for s in range(2)]

        def gather_mark(s, window, row_tag, tag):
            row = pool.tile([P, I], F32, tag=row_tag, name="mark_row%d" % s)
            nc.vector.tensor_copy(row[:], window[:].indirect(offsets[:]))
            turned = bank(tag, "mark_bank%d" % s)
            for r in range(IT):
                nc.tensor.transpose(turned[:, r * P : (r + 1) * P], row[:, r * P : (r + 1) * P], ident[:])
            nc.scalar.copy(marks[s][:], turned[:].rearrange("p (r m) -> p r m", m=P)[:, :, 0])

        interleave_query(0)
        nc.vector.tensor_copy(ks[:], ks_pool[:].indirect(offsets[:]))
        gather_mark(0, x_pool, "xrow", "d0")
        quantize_query(0)
        os_col = pool.tile([P, IT], F32, tag="grp0", name="os_col", align_bytes=64)
        nc.scalar.dma_start(os_col[:], slot_factor.rearrange("o (p c) -> p (o c)", c=IT))
        lam_col = pool.tile([P, QT], F32, tag="xrow", name="lam_col")
        with nc.allow_non_contiguous_dma(reason="one value a partition"):
            nc.scalar.dma_start(lam_col[:], lam.rearrange("(c p) o -> p (c o)", p=P))
        kw = pool.tile([P, I], U32, tag="wx", name="kw", align_bytes=64)
        nc.vector.tensor_copy(kw[:], kw_pool[:].indirect(offsets[:]))
        interleave_query(1)

        v_pool = []

        def load_values(b):
            window = pool.tile([P, T], F32, tag="w%d" % b, name="v_pool%d" % b)
            nc.sync.dma_start(window[:], vals[b * P : (b + 1) * P, :])
            v_pool.append(window)

        sq = [[keep.tile([P, Q], F32, name="sq%d_%d" % (s, r)) for r in range(IT)] for s in range(2)]

        def scores(s):
            banks = [bank("s%d" % (2 * s + h), "score%d_%d" % (s, h)) for h in range(2)]
            for r in range(IT):
                nc.tensor.matmul_mx(
                    out=banks[r // 2][:, (r % 2) * Q : (r % 2 + 1) * Q],
                    lhsT=kw[:, r * P : (r + 1) * P].bitcast(FP8X4),
                    lhsT_scale=ks[:, r * P : (r + 1) * P],
                    rhs=q_codes[s][:].bitcast(FP8X4),
                    rhs_scale=q_scales[s][:],
                    start=True,
                    stop=True,
                )
            for r in range(IT):
                nc.scalar.activation(
                    sq[s][r][:],
                    banks[r // 2][:, (r % 2) * Q : (r % 2 + 1) * Q],
                    ACT.Square,
                    bias=marks[s][:, r : r + 1],
                    scale=-1.0,
                )

        load_values(0)
        load_values(1)
        scores(0)
        gather_mark(1, y_pool, "w3", "u")
        quantize_query(1)
        mem_col = pool.tile([P, QT], F32, tag="grp1", name="mem_col", align_bytes=64)
        nc.sync.dma_start(mem_col[:], memq.rearrange("o (p c) -> p (o c)", c=QT))
        lam_neg = keep.tile([P, 2, QT], F32, name="lam_neg")
        nc.vector.tensor_scalar(lam_neg[:, 0, :], lam_col[:], -1.0, None, ALU.mult)
        nc.vector.tensor_scalar(lam_neg[:, 1, :], lam_col[:], -2.0, None, ALU.mult)
        load_values(2)
        load_values(3)
        scores(1)
        dist = [bank("d%d" % t, "dist%d" % t) for t in range(QT)]
        for s in range(2):
            for r in range(IT):
                for t in range(QT):
                    nc.tensor.matmul(
                        dist[t][:, r * P : (r + 1) * P],
                        sq[s][r][:, t * P : (t + 1) * P],
                        ident[:],
                        start=(s == 0 and r == 0),
                        stop=(s == 1 and r == IT - 1),
                        is_transpose=True,
                    )

        os_bank = bank("s3", "os_bank")
        for c in range(IT):
            nc.tensor.transpose(os_bank[:, c * P : (c + 1) * P], os_col[:, c : c + 1].to_broadcast([P, P]), ident[:])


        def turn_words(tiles, turned, grouped):
            for n, rows in enumerate(tiles):
                words = rows[:].bitcast(F32)
                for u in range(2):
                    cols = slice((2 * n + u) * P, (2 * n + u + 1) * P)
                    nc.tensor.transpose(turned[:, cols], words[:, u : 2 * P : 2], ident[:])
            nc.scalar.copy(
                grouped.bitcast(F32).rearrange("p (n c u) -> p n c u", u=2, c=P),
                turned[:, 0 : 2 * P * len(tiles)].rearrange("p (n u c) -> p n c u", u=2, c=P),
            )

        picked = [keep.tile([P, I], BF16, name="picked%d" % b) for b in range(ET)]
        for b in range(ET):
            nc.vector.tensor_copy(picked[b][:], v_pool[b][:].indirect(offsets[:]))

        p1 = pool.tile([P, RUN, QT * G], F32, tag="p1", name="p1", align_bytes=64)
        p2 = [pool.tile([P, I], F32, tag="p2_%d" % t, name="p2_%d" % t) for t in range(QT)]
        for t in range(QT):
            nc.scalar.activation(
                p1[:, :, t * G : (t + 1) * G],
                dist[t][:].rearrange("p (g j) -> p j g", j=RUN),
                ACT.Exp,
                scale=lam_neg[:, 0, t : t + 1],
            )
        for t in range(QT):
            nc.scalar.activation(p2[t][:], dist[t][:], ACT.Exp, scale=lam_neg[:, 1, t : t + 1])

        sums_turned = bank("s0", "sums_turned")
        for j in range(RUN):
            nc.tensor.matmul(
                sums_turned[:, 0:P], p1[:, j, :], ident[:], start=(j == 0), stop=(j == RUN - 1), is_transpose=True
            )
        sums_staged = pool.tile([P, P], F32, tag="staged", name="sums_staged", align_bytes=64)
        nc.vector.tensor_copy(sums_staged[:], sums_turned[:, 0:P])
        pg_bank = bank("s1", "pg_bank")
        nc.tensor.transpose(pg_bank[:, 0:P], sums_staged[:], ident[:])
        pg = pg_bank[:, 0:P].rearrange("p (t g) -> p t g", g=G)
        inv_root = keep.tile([P, QT, G], F32, name="inv_root")
        nc.scalar.activation(inv_root[:], pg, ACT.Abs_reciprocal_sqrt)
        inv_pg = keep.tile([P, QT, G], F32, name="inv_pg")
        nc.scalar.activation(inv_pg[:], inv_root[:], ACT.Square)
        v_grp = pool.tile([P, E * PACK], BF16, tag="staged", name="v_grp", align_bytes=64)
        for h, tag in enumerate(("s0", "d1")):
            turn_words(picked[2 * h : 2 * h + 2], bank(tag, "v_bank%d" % h), v_grp[:, h * 2 * I : (h + 1) * 2 * I])
        p2os = pool.tile([P, QT, I], F32, tag="p1", name="p2os", align_bytes=64)
        for t in range(QT):
            nc.vector.tensor_tensor(
                p2os[:, t, :].rearrange("m (p c) -> m p c", c=IT),
                p2[t][:].rearrange("m (p c) -> m p c", c=IT),
                os_bank[:].rearrange("m (c p) -> m p c", c=IT),
                ALU.mult,
            )

        root = keep.tile([P, QT, G], F32, name="root")
        root_sum = keep.tile([P, QT], F32, name="root_sum")
        nc.vector.tensor_tensor(root[:], pg, inv_root[:], ALU.mult)
        factor = keep.tile([P, QT, G], F32, name="factor")
        nc.vector.tensor_tensor(factor[:], inv_pg[:], inv_root[:], ALU.mult)
        nc.vector.tensor_reduce(root_sum[:], root[:], AXIS.X, ALU.add)
        inv_sum = keep.tile([P, QT], F32, name="inv_sum")
        nc.vector.reciprocal(inv_sum[:], root_sum[:])

        mem_bank = bank("s1", "mem_bank")
        for c in range(QT):
            nc.tensor.transpose(mem_bank[:, c * P : (c + 1) * P], mem_col[:, c : c + 1].to_broadcast([P, P]), ident[:])
        mem_row = keep.tile([P, Q], F32, name="mem_row")
        nc.scalar.copy(
            mem_row[:].rearrange("m (p c) -> m p c", c=QT),
            mem_bank[:, 0:Q].rearrange("m (c p) -> m p c", c=QT),
        )
        w_grp = [keep.tile([P, P * PACK], BF16, name="w_grp%d" % t, align_bytes=64) for t in range(QT)]
        for t in range(QT):
            weights = keep.tile([P, I], BF16, name="weights%d" % t)
            nc.vector.scalar_tensor_tensor(
                weights[:].rearrange("p (g j) -> p g j", j=RUN),
                p2os[:, t, :].rearrange("p (g j) -> p g j", j=RUN),
                inv_sum[:, t : t + 1],
                factor[:, t, :].unsqueeze(2).to_broadcast([P, G, RUN]),
                ALU.mult,
                ALU.mult,
            )
            turn_words([weights], bank("s%d" % (2 + t), "w_bank%d" % t), w_grp[t][:])
        v_codes = pool.tile([P, E], U32, tag="p1", name="v_codes", align_bytes=64)
        v_scales = keep.tile([P, E], U8, name="v_scales", align_bytes=64)
        nc.vector.quantize_mx(out=v_codes[:].bitcast(FP8X4), scales=v_scales[:], in_=v_grp[:])
        result = keep.tile([P, ET, Q], F32, name="result")
        for t in range(QT):
            w_codes = keep.tile([P, P], U32, name="w_codes%d" % t, align_bytes=64)
            w_scales = keep.tile([P, P], U8, name="w_scales%d" % t, align_bytes=64)
            nc.vector.quantize_mx(
                out=w_codes[:].bitcast(FP8X4), scales=w_scales[:], in_=w_grp[t][:]
            )
            halves = [slice(h * HALF, (h + 1) * HALF) for h in range(2)]
            sums = []
            for half, tag in zip(halves, (("t", "u"), ("d0", "s0"))[t]):
                acc = bank(tag, "acc%d_%d" % (t, half.start))
                for n, b in enumerate(range(half.start, half.stop)):
                    nc.tensor.matmul_mx(
                        out=acc[:, n * P : (n + 1) * P],
                        lhsT=v_codes[:, b * P : (b + 1) * P].bitcast(FP8X4),
                        lhsT_scale=v_scales[:, b * P : (b + 1) * P],
                        rhs=w_codes[:].bitcast(FP8X4),
                        rhs_scale=w_scales[:],
                        start=True,
                        stop=True,
                    )
                sums.append(acc[:, 0 : HALF * P].rearrange("p (b q) -> p b q", b=HALF))
            first = t * P + 1
            count = min(P, Q - first)
            for half, part in zip(halves, sums):
                nc.vector.tensor_tensor(
                    carried[:, half, first : first + count],
                    part[:, :, 0:count],
                    mem_row[:, first : first + count].unsqueeze(1).to_broadcast([P, HALF, count]),
                    ALU.mult,
                )
            for half, part, queue in zip(halves, sums, (nc.sync, nc.scalar if t == QT - 1 else nc.sync)):
                cols = slice(t * P, (t + 1) * P)
                nc.vector.tensor_tensor(result[:, half, cols], part, carried[:, half, cols], ALU.subtract)
                queue.dma_start(out.rearrange("(b p) q -> p b q", p=P)[:, half, cols], result[:, half, cols])
